import numpy as np
import ml_dtypes


def mxq(x, axis, fmt="e4m3"):
    dtype, down = {"e4m3": (ml_dtypes.float8_e4m3fn, 7), "e5m2": (ml_dtypes.float8_e5m2, 14)}[fmt]
    v = np.moveaxis(np.asarray(x, np.float32).astype(ml_dtypes.bfloat16).astype(np.float64), axis, -1)
    blocks = v.reshape(v.shape[:-1] + (-1, 32))
    amax = np.abs(blocks).max(-1, keepdims=True)
    byte = np.maximum(np.where(amax > 0, np.frexp(amax)[1] - 1 + 127, 0) - down, 1)
    scale = np.exp2(byte - 127.0)
    codes = (blocks / scale).astype(np.float32).astype(dtype).astype(np.float64)
    return np.moveaxis((codes * scale).reshape(v.shape), -1, axis)


WIDE = False


def mx_kscale(k):
    if not WIDE:
        return np.ones(k)
    levels = np.array([10, -10, 5, -5, 0])
    if k % 512:
        return np.exp2(np.random.permutation(np.resize(levels, k // 32))).repeat(32)
    a = np.empty((k // 512, 16))
    for p in range(k // 512):
        a[p, :8] = np.random.permutation(np.resize(levels, 8))
        for g in range(8):
            far = levels[np.abs(levels - a[p, g]) >= 10]
            a[p, g + 8] = far[np.random.randint(len(far))]
    return np.exp2(a.ravel()).repeat(32)


def f64(x):
    return np.asarray(x).astype(np.float64)


def striped8(idx):
    return np.concatenate([v.reshape(-1, 16).T for v in idx]).astype(np.uint16)


def unstriped8(offs):
    return np.stack([offs[16 * g:16 * g + 16].T.reshape(-1) for g in range(8)]).astype(np.int64)


E2M1 = np.array([0.0, 0.5, 1.0, 1.5, 2.0, 3.0, 4.0, 6.0, -0.0, -0.5, -1.0, -1.5, -2.0, -3.0, -4.0, -6.0])


def pack_weight(w, fmt):
    k, n = w.shape
    w = f64(np.asarray(w, np.float32).astype(ml_dtypes.bfloat16)).reshape(k // 32, 32, n)
    amax = np.abs(w).max(1)
    if fmt == "e4m3":
        byte = np.frexp(amax)[1] - 1 + 127 - 7
    else:
        mant, ex = np.frexp(amax / 6.0)
        byte = np.where(mant > 0.5, ex, ex - 1) + 127
    byte = np.clip(np.where(amax > 0, byte, 1), 1, 254)
    scaled = (w * np.exp2(127.0 - byte)[:, None, :]).reshape(k, n).astype(np.float32)
    by_word = np.ascontiguousarray(scaled.reshape(k // 512, 128, 4, n).transpose(0, 1, 3, 2))
    if fmt == "e4m3":
        words = by_word.astype(ml_dtypes.float8_e4m3fn).view(np.uint8)
    else:
        c = by_word.astype(ml_dtypes.float4_e2m1fn).view(np.uint8) & 0xF
        words = (c[..., 0::2] | (c[..., 1::2] << 4)).reshape(k // 512, 128, 2 * n)
    return np.ascontiguousarray(words), np.ascontiguousarray(byte.astype(np.uint8).reshape(k // 512, 16, n))


def unpack_weight(words, scales, fmt):
    g, _, n = scales.shape
    words = np.ascontiguousarray(words).reshape(g, 128, n, -1)
    if fmt == "e4m3":
        vals = words.view(ml_dtypes.float8_e4m3fn).astype(np.float64)
    else:
        nib = np.empty((g, 128, n, 4), np.uint8)
        nib[..., 0::2] = words & 0xF
        nib[..., 1::2] = words >> 4
        vals = E2M1[nib]
    vals = vals * np.repeat(np.exp2(scales.astype(np.float64) - 127.0), 8, axis=1)[..., None]
    return vals.transpose(0, 1, 3, 2).reshape(g * 512, n)


K, M, T, S = 1536, 512, 4096, 2048


def setup_inputs():
    n = np.random.standard_normal
    s = mx_kscale(K)[:, None]
    p_w = pack_weight(n((K, M)) / np.sqrt(K) / s, "e4m3")
    return {
        "x": (n((K, S)) * s).astype(np.float32),
        "w_words": p_w[0],
        "w_scales": p_w[1],
        "wgo": np.repeat(np.random.uniform(0.5, 2.0, (8, S)), 16, axis=0).astype(np.float32),
        "offs": striped8(np.stack([np.random.permutation(T)[:S] for _ in range(8)])),
    }


def reference(x, w_words, w_scales, wgo, offs):
    x_ = mxq(f64(x), 0, "e4m3")
    w_ = unpack_weight(w_words, w_scales, "e4m3")
    y = w_.T @ x_
    place = unstriped8(offs)[np.arange(M) % 128 // 16]
    out = np.zeros((M, T))
    out[np.arange(M)[:, None], place] = f64(wgo)[np.arange(M) % 128] * (y)
    return out

@@ -1,0 +1,159 @@
+from contextlib import ExitStack
+
+import concourse.mybir as mybir
+
+F32 = mybir.dt.float32
+BF16 = mybir.dt.bfloat16
+I32 = mybir.dt.int32
+U32 = mybir.dt.uint32
+U16 = mybir.dt.uint16
+U8 = mybir.dt.uint8
+FP8X4 = mybir.dt.float8_e4m3fn_x4
+MULT = mybir.AluOpType.mult
+
+K, M, T, S = 1536, 512, 4096, 2048
+P = 128
+PASSES = K // 512
+BLOCKS = M // P
+HALF = S // 2
+CHUNK = 512
+FLOPS = 2 * K * M * S
+
+
+def interleave(copy, grouped, raw, c0, c1):
+    copy(
+        out=grouped[:, c0:c1, :].rearrange("p (c i) t -> p c t i", i=4),
+        in_=raw[:, :, c0:c1].rearrange("p t (c i) -> p c t i", i=4),
+    )
+
+
+def tile_list_hscat_none_kernel(tc, x, w_words, w_scales, wgo, offs, out):
+    nc = tc.nc
+    with ExitStack() as ctx:
+        keep = ctx.enter_context(tc.tile_pool(name="keep", bufs=1))
+        stage = ctx.enter_context(tc.tile_pool(name="stage", bufs=9))
+        group = ctx.enter_context(tc.tile_pool(name="group", bufs=4))
+        ypool = ctx.enter_context(tc.tile_pool(name="ypool", bufs=6))
+        psum = ctx.enter_context(tc.psum_pool(name="psum", bufs=8))
+
+        offsets = keep.tile([P, S // 16], U16, name="offsets")
+        nc.sync.dma_start(offsets[:], offs)
+
+        ws = keep.tile([P, PASSES, M], U8, name="ws", align_bytes=64)
+        nc.vector.memset(ws[:].bitcast(I32), 0)
+        rows = w_scales.rearrange("a q n -> q a n")
+        for q in range(4):
+            nc.scalar.dma_start(ws[32 * q : 32 * q + 4, :, :].bitcast(I32), rows[4 * q : 4 * q + 4, :, :].bitcast(I32))
+
+        words = w_words.rearrange("a p n t -> p a (n t)")
+        w_first = keep.tile([P, PASSES, P], U32, name="w_first", align_bytes=64)
+        w_rest = keep.tile([P, PASSES, M - P], U32, name="w_rest", align_bytes=64)
+        wgo_half = [keep.tile([P, HALF], F32, name=f"wgo{h}") for h in range(2)]
+        windows = [keep.tile([P, T], F32, name=f"window{b}") for b in range(BLOCKS)]
+
+        def weights(a, b):
+            if b == 0:
+                return w_first[:, a, :].bitcast(FP8X4)
+            return w_rest[:, a, P * (b - 1) : P * b].bitcast(FP8X4)
+
+        codes = {}
+        scales = {}
+        for h in range(2):
+            for c in range(2):
+                for a in range(PASSES):
+                    codes[h, c, a] = keep.tile([P, CHUNK], U32, name=f"codes{h}{c}{a}", align_bytes=64)
+                    scales[h, c, a] = keep.tile([P, CHUNK], U8, name=f"scales{h}{c}{a}", align_bytes=64)
+
+        raws = {}
+
+        def load(h, c, a, parts=1):
+            raw = stage.tile([P, 4, CHUNK], F32, name="raw")
+            width = CHUNK // parts
+            src = x[512 * a : 512 * (a + 1), h * HALF + c * CHUNK : h * HALF + (c + 1) * CHUNK].rearrange("(p j) w -> p j w", j=4)
+            for s in range(parts):
+                cols = slice(s * width, (s + 1) * width)
+                nc.sync.dma_start(raw[:, :, cols], src[:, :, cols])
+            raws[h, c, a] = raw
+
+        def quantise(h, c, a, scalar_share, parts=1):
+            raw = raws[h, c, a]
+            grouped = group.tile([P, CHUNK, 4], BF16, name="grouped", align_bytes=64)
+            width = CHUNK // parts
+            for s in range(parts):
+                lo, hi = s * width, (s + 1) * width
+                cut = lo + scalar_share
+                if scalar_share:
+                    interleave(nc.scalar.copy, grouped, raw, lo, cut)
+                if cut < hi:
+                    interleave(nc.vector.tensor_copy, grouped, raw, cut, hi)
+                nc.vector.quantize_mx(
+                    out=codes[h, c, a][:, lo:hi].bitcast(FP8X4),
+                    scales=scales[h, c, a][:, lo:hi],
+                    in_=grouped[:, lo:hi, :].rearrange("p w t -> p (w t)"),
+                )
+
+        def product(h, c, b, y, lo, hi):
+            acc = psum.tile([P, CHUNK], F32, name="acc")
+            for a in range(PASSES):
+                nc.tensor.matmul_mx(
+                    out=acc[:, : hi - lo],
+                    lhsT=weights(a, b),
+                    lhsT_scale=ws[:, a, P * b : P * (b + 1)],
+                    rhs=codes[h, c, a][:, lo:hi].bitcast(FP8X4),
+                    rhs_scale=scales[h, c, a][:, lo:hi],
+                    start=(a == 0),
+                    stop=(a == PASSES - 1),
+                )
+            nc.scalar.copy(out=y[:, c * CHUNK + lo : c * CHUNK + hi], in_=acc[:, : hi - lo])
+
+        def place(h, b, y):
+            cols = slice(h * HALF // 16, (h + 1) * HALF // 16)
+            nc.vector.tensor_tensor(windows[b][:].indirect(offsets[:, cols]), y[:], wgo_half[h][:], MULT)
+
+        load(0, 0, 0)
+        nc.sync.dma_start(w_first[:].bitcast(I32), words[:, :, : 4 * P].bitcast(I32))
+        load(0, 0, 1)
+        load(0, 0, 2)
+        load(0, 1, 0)
+        load(0, 1, 1)
+        load(0, 1, 2, parts=2)
+        nc.sync.dma_start(wgo_half[0][:], wgo[:, :HALF])
+        nc.sync.dma_start(w_rest[:].bitcast(I32), words[:, :, 4 * P :].bitcast(I32))
+
+        for q in range(4):
+            nc.vector.memset(windows[0][:, q * 1024 : (q + 1) * 1024], 0.0)
+
+        ys = {}
+        ys[0, 0] = ypool.tile([P, HALF], F32, name="y")
+        for a in range(PASSES):
+            quantise(0, 0, a, 352)
+        product(0, 0, 0, ys[0, 0], 0, CHUNK)
+        for a in range(2):
+            quantise(0, 1, a, 352)
+        quantise(0, 1, 2, 96, parts=2)
+        for lo in (0, 256):
+            product(0, 1, 0, ys[0, 0], lo, lo + 256)
+        for b in range(1, BLOCKS):
+            for q in range(4):
+                nc.vector.memset(windows[b][:, q * 1024 : (q + 1) * 1024], 0.0)
+        place(0, 0, ys[0, 0])
+
+        for c in range(2):
+            for a in range(PASSES):
+                load(1, c, a)
+        nc.sync.dma_start(wgo_half[1][:], wgo[:, HALF:])
+
+        for b in range(1, BLOCKS):
+            ys[0, b] = ypool.tile([P, HALF], F32, name="y")
+            for c in range(2):
+                product(0, c, b, ys[0, b], 0, CHUNK)
+            if b >= 2:
+                for a in range(PASSES):
+                    quantise(1, b - 2, a, CHUNK)
+            place(0, b, ys[0, b])
+        for b in range(BLOCKS):
+            ys[1, b] = ypool.tile([P, HALF], F32, name="y")
+            for c in range(2):
+                product(1, c, b, ys[1, b], 0, CHUNK)
+            place(1, b, ys[1, b])
+            nc.sync.dma_start(out[P * b : P * (b + 1), :], windows[b][:])

@@ -20,10 +20,10 @@ CHUNK = 512
 FLOPS = 2 * K * M * S
 
 
-def interleave(copy, grouped, raw, c0, c1):
+def interleave(copy, grouped, raw, to, start, n):
     copy(
-        out=grouped[:, c0:c1, :].rearrange("p (c i) t -> p c t i", i=4),
-        in_=raw[:, :, c0:c1].rearrange("p t (c i) -> p c t i", i=4),
+        out=grouped[:, to : to + n, :].rearrange("p (c i) t -> p c t i", i=4),
+        in_=raw[:, :, start : start + n].rearrange("p t (c i) -> p c t i", i=4),
     )
 
 
@@ -31,30 +31,21 @@ def tile_list_hscat_none_kernel(tc, x, w_words, w_scales, wgo, offs, out):
     nc = tc.nc
     with ExitStack() as ctx:
         keep = ctx.enter_context(tc.tile_pool(name="keep", bufs=1))
-        stage = ctx.enter_context(tc.tile_pool(name="stage", bufs=9))
-        group = ctx.enter_context(tc.tile_pool(name="group", bufs=4))
+        stage = ctx.enter_context(tc.tile_pool(name="stage", bufs=3))
+        small = ctx.enter_context(tc.tile_pool(name="small", bufs=2))
+        group = ctx.enter_context(tc.tile_pool(name="group", bufs=8))
         ypool = ctx.enter_context(tc.tile_pool(name="ypool", bufs=6))
         psum = ctx.enter_context(tc.psum_pool(name="psum", bufs=8))
 
         offsets = keep.tile([P, S // 16], U16, name="offsets")
-        nc.sync.dma_start(offsets[:], offs)
-
         ws = keep.tile([P, PASSES, M], U8, name="ws", align_bytes=64)
-        nc.vector.memset(ws[:].bitcast(I32), 0)
-        rows = w_scales.rearrange("a q n -> q a n")
-        for q in range(4):
-            nc.scalar.dma_start(ws[32 * q : 32 * q + 4, :, :].bitcast(I32), rows[4 * q : 4 * q + 4, :, :].bitcast(I32))
-
         words = w_words.rearrange("a p n t -> p a (n t)")
-        w_first = keep.tile([P, PASSES, P], U32, name="w_first", align_bytes=64)
-        w_rest = keep.tile([P, PASSES, M - P], U32, name="w_rest", align_bytes=64)
+        w_block = [keep.tile([P, PASSES, P], U32, name=f"w{b}", align_bytes=64) for b in range(BLOCKS)]
         wgo_half = [keep.tile([P, HALF], F32, name=f"wgo{h}") for h in range(2)]
         windows = [keep.tile([P, T], F32, name=f"window{b}") for b in range(BLOCKS)]
 
-        def weights(a, b):
-            if b == 0:
-                return w_first[:, a, :].bitcast(FP8X4)
-            return w_rest[:, a, P * (b - 1) : P * b].bitcast(FP8X4)
+        def load_weights(b):
+            nc.sync.dma_start(w_block[b][:].bitcast(I32), words[:, :, 4 * P * b : 4 * P * (b + 1)].bitcast(I32))
 
         codes = {}
         scales = {}
@@ -64,96 +55,100 @@ def tile_list_hscat_none_kernel(tc, x, w_words, w_scales, wgo, offs, out):
                     codes[h, c, a] = keep.tile([P, CHUNK], U32, name=f"codes{h}{c}{a}", align_bytes=64)
                     scales[h, c, a] = keep.tile([P, CHUNK], U8, name=f"scales{h}{c}{a}", align_bytes=64)
 
-        raws = {}
+        def load(h, a, lo, hi, pool=stage):
+            raw = pool.tile([P, 4, hi - lo], F32, name="raw")
+            src = x[512 * a : 512 * (a + 1), h * HALF + lo : h * HALF + hi].rearrange("(p j) w -> p j w", j=4)
+            nc.sync.dma_start(raw[:], src)
+            return raw
 
-        def load(h, c, a, parts=1):
-            raw = stage.tile([P, 4, CHUNK], F32, name="raw")
-            width = CHUNK // parts
-            src = x[512 * a : 512 * (a + 1), h * HALF + c * CHUNK : h * HALF + (c + 1) * CHUNK].rearrange("(p j) w -> p j w", j=4)
-            for s in range(parts):
-                cols = slice(s * width, (s + 1) * width)
-                nc.sync.dma_start(raw[:, :, cols], src[:, :, cols])
-            raws[h, c, a] = raw
-
-        def quantise(h, c, a, scalar_share, parts=1):
-            raw = raws[h, c, a]
+        def quantise(h, a, raw, raw_lo, lo, hi, scalar_share):
             grouped = group.tile([P, CHUNK, 4], BF16, name="grouped", align_bytes=64)
-            width = CHUNK // parts
-            for s in range(parts):
-                lo, hi = s * width, (s + 1) * width
-                cut = lo + scalar_share
-                if scalar_share:
-                    interleave(nc.scalar.copy, grouped, raw, lo, cut)
-                if cut < hi:
-                    interleave(nc.vector.tensor_copy, grouped, raw, cut, hi)
-                nc.vector.quantize_mx(
-                    out=codes[h, c, a][:, lo:hi].bitcast(FP8X4),
-                    scales=scales[h, c, a][:, lo:hi],
-                    in_=grouped[:, lo:hi, :].rearrange("p w t -> p (w t)"),
-                )
+            n = hi - lo
+            if scalar_share:
+                interleave(nc.scalar.copy, grouped, raw, 0, lo - raw_lo, scalar_share)
+            if scalar_share < n:
+                interleave(nc.vector.tensor_copy, grouped, raw, scalar_share, lo - raw_lo + scalar_share, n - scalar_share)
+            c, start = lo // CHUNK, lo % CHUNK
+            nc.vector.quantize_mx(
+                out=codes[h, c, a][:, start : start + n].bitcast(FP8X4),
+                scales=scales[h, c, a][:, start : start + n],
+                in_=grouped[:, :n, :].rearrange("p w t -> p (w t)"),
+            )
 
-        def product(h, c, b, y, lo, hi):
+        def product(h, b, y, lo, hi):
             acc = psum.tile([P, CHUNK], F32, name="acc")
+            c, start, n = lo // CHUNK, lo % CHUNK, hi - lo
             for a in range(PASSES):
                 nc.tensor.matmul_mx(
-                    out=acc[:, : hi - lo],
-                    lhsT=weights(a, b),
+                    out=acc[:, :n],
+                    lhsT=w_block[b][:, a, :].bitcast(FP8X4),
                     lhsT_scale=ws[:, a, P * b : P * (b + 1)],
-                    rhs=codes[h, c, a][:, lo:hi].bitcast(FP8X4),
-                    rhs_scale=scales[h, c, a][:, lo:hi],
+                    rhs=codes[h, c, a][:, start : start + n].bitcast(FP8X4),
+                    rhs_scale=scales[h, c, a][:, start : start + n],
                     start=(a == 0),
                     stop=(a == PASSES - 1),
                 )
-            nc.scalar.copy(out=y[:, c * CHUNK + lo : c * CHUNK + hi], in_=acc[:, : hi - lo])
+            nc.scalar.copy(out=y[:, lo:hi], in_=acc[:, :n])
+
+        def blank(b, memset):
+            for q in range(4):
+                memset(windows[b][:, q * 1024 : (q + 1) * 1024].bitcast(I32), 0)
 
         def place(h, b, y):
             cols = slice(h * HALF // 16, (h + 1) * HALF // 16)
             nc.vector.tensor_tensor(windows[b][:].indirect(offsets[:, cols]), y[:], wgo_half[h][:], MULT)
 
-        load(0, 0, 0)
-        nc.sync.dma_start(w_first[:].bitcast(I32), words[:, :, : 4 * P].bitcast(I32))
-        load(0, 0, 1)
-        load(0, 0, 2)
-        load(0, 1, 0)
-        load(0, 1, 1)
-        load(0, 1, 2, parts=2)
-        nc.sync.dma_start(wgo_half[0][:], wgo[:, :HALF])
-        nc.sync.dma_start(w_rest[:].bitcast(I32), words[:, :, 4 * P :].bitcast(I32))
-
+        nc.vector.memset(ws[:].bitcast(I32), 0)
+        rows = w_scales.rearrange("a q n -> q a n")
         for q in range(4):
-            nc.vector.memset(windows[0][:, q * 1024 : (q + 1) * 1024], 0.0)
+            nc.scalar.dma_start(ws[32 * q : 32 * q + 4, :, :].bitcast(I32), rows[4 * q : 4 * q + 4, :, :].bitcast(I32))
+        blank(0, nc.gpsimd.memset)
+        blank(1, nc.vector.memset)
+
+        raw_a = [load(0, 0, 0, HALF)]
+        load_weights(0)
+        nc.sync.dma_start(offsets[:], offs)
+        raw_a.append(load(0, 1, 0, HALF))
+        last_pieces = [(0, 512), (512, 768), (768, 1024)]
+        raw_last = [load(0, 2, lo, hi, small if lo >= 512 else stage) for lo, hi in last_pieces]
+        nc.sync.dma_start(wgo_half[0][:], wgo[:, :HALF])
+        load_weights(1)
 
         ys = {}
         ys[0, 0] = ypool.tile([P, HALF], F32, name="y")
-        for a in range(PASSES):
-            quantise(0, 0, a, 352)
-        product(0, 0, 0, ys[0, 0], 0, CHUNK)
         for a in range(2):
-            quantise(0, 1, a, 352)
-        quantise(0, 1, 2, 96, parts=2)
-        for lo in (0, 256):
-            product(0, 1, 0, ys[0, 0], lo, lo + 256)
-        for b in range(1, BLOCKS):
-            for q in range(4):
-                nc.vector.memset(windows[b][:, q * 1024 : (q + 1) * 1024], 0.0)
+            for lo in (0, 512):
+                quantise(0, a, raw_a[a], 0, lo, lo + 512, 384)
+        for (lo, hi), raw, share in zip(last_pieces, raw_last, (384, 128, 80)):
+            quantise(0, 2, raw, lo, lo, hi, share)
+            product(0, 0, ys[0, 0], lo, hi)
         place(0, 0, ys[0, 0])
 
-        for c in range(2):
-            for a in range(PASSES):
-                load(1, c, a)
-        nc.sync.dma_start(wgo_half[1][:], wgo[:, HALF:])
+        blank(2, nc.vector.memset)
+        blank(3, nc.vector.memset)
 
-        for b in range(1, BLOCKS):
-            ys[0, b] = ypool.tile([P, HALF], F32, name="y")
-            for c in range(2):
-                product(0, c, b, ys[0, b], 0, CHUNK)
-            if b >= 2:
-                for a in range(PASSES):
-                    quantise(1, b - 2, a, CHUNK)
-            place(0, b, ys[0, b])
+        raw_b = [load(1, 0, 0, HALF), load(1, 1, 0, HALF)]
+        load_weights(2)
+        raw_b.append(load(1, 2, 0, HALF))
+        nc.sync.dma_start(wgo_half[1][:], wgo[:, HALF:])
+        load_weights(3)
+
+        def products(h, b):
+            y = ypool.tile([P, HALF], F32, name="y")
+            for lo in (0, 512):
+                product(h, b, y, lo, lo + 512)
+            place(h, b, y)
+
+        def quantise_b(a):
+            for lo in (0, 512):
+                quantise(1, a, raw_b[a], 0, lo, lo + 512, 512)
+
+        products(0, 1)
+        quantise_b(0)
+        products(0, 2)
+        quantise_b(1)
+        quantise_b(2)
+        products(0, 3)
         for b in range(BLOCKS):
-            ys[1, b] = ypool.tile([P, HALF], F32, name="y")
-            for c in range(2):
-                product(1, c, b, ys[1, b], 0, CHUNK)
-            place(1, b, ys[1, b])
+            products(1, b)
             nc.sync.dma_start(out[P * b : P * (b + 1), :], windows[b][:])

@@ -31,7 +31,8 @@ def tile_list_hscat_none_kernel(tc, x, w_words, w_scales, wgo, offs, out):
     nc = tc.nc
     with ExitStack() as ctx:
         keep = ctx.enter_context(tc.tile_pool(name="keep", bufs=1))
-        stage = ctx.enter_context(tc.tile_pool(name="stage", bufs=3))
+        stage = ctx.enter_context(tc.tile_pool(name="stage", bufs=2))
+        stage_b = ctx.enter_context(tc.tile_pool(name="stage_b", bufs=4))
         small = ctx.enter_context(tc.tile_pool(name="small", bufs=2))
         group = ctx.enter_context(tc.tile_pool(name="group", bufs=8))
         ypool = ctx.enter_context(tc.tile_pool(name="ypool", bufs=6))
@@ -103,14 +104,15 @@ def tile_list_hscat_none_kernel(tc, x, w_words, w_scales, wgo, offs, out):
         for q in range(4):
             nc.scalar.dma_start(ws[32 * q : 32 * q + 4, :, :].bitcast(I32), rows[4 * q : 4 * q + 4, :, :].bitcast(I32))
         blank(0, nc.gpsimd.memset)
-        blank(1, nc.vector.memset)
+        for b in range(1, BLOCKS):
+            blank(b, nc.vector.memset)
 
         raw_a = [load(0, 0, 0, HALF)]
         load_weights(0)
         nc.sync.dma_start(offsets[:], offs)
         raw_a.append(load(0, 1, 0, HALF))
         last_pieces = [(0, 512), (512, 768), (768, 1024)]
-        raw_last = [load(0, 2, lo, hi, small if lo >= 512 else stage) for lo, hi in last_pieces]
+        raw_last = [load(0, 2, lo, hi, small if lo >= 512 else stage_b) for lo, hi in last_pieces]
         nc.sync.dma_start(wgo_half[0][:], wgo[:, :HALF])
         load_weights(1)
 
@@ -118,18 +120,18 @@ def tile_list_hscat_none_kernel(tc, x, w_words, w_scales, wgo, offs, out):
         ys[0, 0] = ypool.tile([P, HALF], F32, name="y")
         for a in range(2):
             for lo in (0, 512):
-                quantise(0, a, raw_a[a], 0, lo, lo + 512, 384)
-        for (lo, hi), raw, share in zip(last_pieces, raw_last, (384, 128, 80)):
+                quantise(0, a, raw_a[a], 0, lo, lo + 512, 256)
+        for (lo, hi), raw, share in zip(last_pieces, raw_last, (256, 112, 80)):
             quantise(0, 2, raw, lo, lo, hi, share)
             product(0, 0, ys[0, 0], lo, hi)
         place(0, 0, ys[0, 0])
 
-        blank(2, nc.vector.memset)
-        blank(3, nc.vector.memset)
-
-        raw_b = [load(1, 0, 0, HALF), load(1, 1, 0, HALF)]
-        load_weights(2)
-        raw_b.append(load(1, 2, 0, HALF))
+        raw_b = {}
+        for a in range(PASSES):
+            for lo in (0, 512):
+                raw_b[a, lo] = load(1, a, lo, lo + 512, stage_b)
+            if a == 1:
+                load_weights(2)
         nc.sync.dma_start(wgo_half[1][:], wgo[:, HALF:])
         load_weights(3)
 
@@ -141,7 +143,7 @@ def tile_list_hscat_none_kernel(tc, x, w_words, w_scales, wgo, offs, out):
 
         def quantise_b(a):
             for lo in (0, 512):
-                quantise(1, a, raw_b[a], 0, lo, lo + 512, 512)
+                quantise(1, a, raw_b[a, lo], lo, lo, lo + 512, 512)
 
         products(0, 1)
         quantise_b(0)

from contextlib import ExitStack

import concourse.mybir as mybir

F32 = mybir.dt.float32
BF16 = mybir.dt.bfloat16
I32 = mybir.dt.int32
U32 = mybir.dt.uint32
U16 = mybir.dt.uint16
U8 = mybir.dt.uint8
FP8X4 = mybir.dt.float8_e4m3fn_x4
MULT = mybir.AluOpType.mult

K, M, T, S = 1536, 512, 4096, 2048
P = 128
PASSES = K // 512
BLOCKS = M // P
HALF = S // 2
CHUNK = 512
FLOPS = 2 * K * M * S


def interleave(copy, grouped, raw, to, start, n):
    copy(
        out=grouped[:, to : to + n, :].rearrange("p (c i) t -> p c t i", i=4),
        in_=raw[:, :, start : start + n].rearrange("p t (c i) -> p c t i", i=4),
    )


def tile_list_hscat_none_kernel(tc, x, w_words, w_scales, wgo, offs, out):
    nc = tc.nc
    with ExitStack() as ctx:
        keep = ctx.enter_context(tc.tile_pool(name="keep", bufs=1))
        stage = ctx.enter_context(tc.tile_pool(name="stage", bufs=2))
        stage_b = ctx.enter_context(tc.tile_pool(name="stage_b", bufs=4))
        small = ctx.enter_context(tc.tile_pool(name="small", bufs=2))
        group = ctx.enter_context(tc.tile_pool(name="group", bufs=8))
        ypool = ctx.enter_context(tc.tile_pool(name="ypool", bufs=6))
        psum = ctx.enter_context(tc.psum_pool(name="psum", bufs=8))

        offsets = keep.tile([P, S // 16], U16, name="offsets")
        ws = keep.tile([P, PASSES, M], U8, name="ws", align_bytes=64)
        words = w_words.rearrange("a p n t -> p a (n t)")
        w_block = [keep.tile([P, PASSES, P], U32, name=f"w{b}", align_bytes=64) for b in range(BLOCKS)]
        wgo_half = [keep.tile([P, HALF], F32, name=f"wgo{h}") for h in range(2)]
        windows = [keep.tile([P, T], F32, name=f"window{b}") for b in range(BLOCKS)]

        def load_weights(b):
            nc.sync.dma_start(w_block[b][:].bitcast(I32), words[:, :, 4 * P * b : 4 * P * (b + 1)].bitcast(I32))

        codes = {}
        scales = {}
        for h in range(2):
            for c in range(2):
                for a in range(PASSES):
                    codes[h, c, a] = keep.tile([P, CHUNK], U32, name=f"codes{h}{c}{a}", align_bytes=64)
                    scales[h, c, a] = keep.tile([P, CHUNK], U8, name=f"scales{h}{c}{a}", align_bytes=64)

        def load(h, a, lo, hi, pool=stage):
            raw = pool.tile([P, 4, hi - lo], F32, name="raw")
            src = x[512 * a : 512 * (a + 1), h * HALF + lo : h * HALF + hi].rearrange("(p j) w -> p j w", j=4)
            nc.sync.dma_start(raw[:], src)
            return raw

        def quantise(h, a, raw, raw_lo, lo, hi, scalar_share):
            grouped = group.tile([P, CHUNK, 4], BF16, name="grouped", align_bytes=64)
            n = hi - lo
            if scalar_share:
                interleave(nc.scalar.copy, grouped, raw, 0, lo - raw_lo, scalar_share)
            if scalar_share < n:
                interleave(nc.vector.tensor_copy, grouped, raw, scalar_share, lo - raw_lo + scalar_share, n - scalar_share)
            c, start = lo // CHUNK, lo % CHUNK
            nc.vector.quantize_mx(
                out=codes[h, c, a][:, start : start + n].bitcast(FP8X4),
                scales=scales[h, c, a][:, start : start + n],
                in_=grouped[:, :n, :].rearrange("p w t -> p (w t)"),
            )

        def product(h, b, y, lo, hi):
            acc = psum.tile([P, CHUNK], F32, name="acc")
            c, start, n = lo // CHUNK, lo % CHUNK, hi - lo
            for a in range(PASSES):
                nc.tensor.matmul_mx(
                    out=acc[:, :n],
                    lhsT=w_block[b][:, a, :].bitcast(FP8X4),
                    lhsT_scale=ws[:, a, P * b : P * (b + 1)],
                    rhs=codes[h, c, a][:, start : start + n].bitcast(FP8X4),
                    rhs_scale=scales[h, c, a][:, start : start + n],
                    start=(a == 0),
                    stop=(a == PASSES - 1),
                )
            nc.scalar.copy(out=y[:, lo:hi], in_=acc[:, :n])

        def blank(b, memset):
            for q in range(4):
                memset(windows[b][:, q * 1024 : (q + 1) * 1024].bitcast(I32), 0)

        def place(h, b, y):
            cols = slice(h * HALF // 16, (h + 1) * HALF // 16)
            nc.vector.tensor_tensor(windows[b][:].indirect(offsets[:, cols]), y[:], wgo_half[h][:], MULT)

        nc.vector.memset(ws[:].bitcast(I32), 0)
        rows = w_scales.rearrange("a q n -> q a n")
        for q in range(4):
            nc.scalar.dma_start(ws[32 * q : 32 * q + 4, :, :].bitcast(I32), rows[4 * q : 4 * q + 4, :, :].bitcast(I32))
        blank(0, nc.gpsimd.memset)
        for b in range(1, BLOCKS):
            blank(b, nc.vector.memset)

        raw_a = [load(0, 0, 0, HALF)]
        load_weights(0)
        nc.sync.dma_start(offsets[:], offs)
        raw_a.append(load(0, 1, 0, HALF))
        last_pieces = [(0, 512), (512, 768), (768, 1024)]
        raw_last = [load(0, 2, lo, hi, small if lo >= 512 else stage_b) for lo, hi in last_pieces]
        nc.sync.dma_start(wgo_half[0][:], wgo[:, :HALF])
        load_weights(1)

        ys = {}
        ys[0, 0] = ypool.tile([P, HALF], F32, name="y")
        for a in range(2):
            for lo in (0, 512):
                quantise(0, a, raw_a[a], 0, lo, lo + 512, 256)
        for (lo, hi), raw, share in zip(last_pieces, raw_last, (256, 112, 80)):
            quantise(0, 2, raw, lo, lo, hi, share)
            product(0, 0, ys[0, 0], lo, hi)
        place(0, 0, ys[0, 0])

        raw_b = {}
        for a in range(PASSES):
            for lo in (0, 512):
                raw_b[a, lo] = load(1, a, lo, lo + 512, stage_b)
            if a == 1:
                load_weights(2)
        nc.sync.dma_start(wgo_half[1][:], wgo[:, HALF:])
        load_weights(3)

        def products(h, b):
            y = ypool.tile([P, HALF], F32, name="y")
            for lo in (0, 512):
                product(h, b, y, lo, lo + 512)
            place(h, b, y)

        def quantise_b(a):
            for lo in (0, 512):
                quantise(1, a, raw_b[a, lo], lo, lo, lo + 512, 512)

        products(0, 1)
        quantise_b(0)
        products(0, 2)
        quantise_b(1)
        quantise_b(2)
        products(0, 3)
        for b in range(BLOCKS):
            products(1, b)
            nc.sync.dma_start(out[P * b : P * (b + 1), :], windows[b][:])
